import numpy as np
import ml_dtypes


def mxq(x, axis, fmt="e4m3"):
    dtype, down = {"e4m3": (ml_dtypes.float8_e4m3fn, 7), "e5m2": (ml_dtypes.float8_e5m2, 14)}[fmt]
    v = np.moveaxis(np.asarray(x, np.float32).astype(ml_dtypes.bfloat16).astype(np.float64), axis, -1)
    blocks = v.reshape(v.shape[:-1] + (-1, 32))
    amax = np.abs(blocks).max(-1, keepdims=True)
    byte = np.maximum(np.where(amax > 0, np.frexp(amax)[1] - 1 + 127, 0) - down, 1)
    scale = np.exp2(byte - 127.0)
    codes = (blocks / scale).astype(np.float32).astype(dtype).astype(np.float64)
    return np.moveaxis((codes * scale).reshape(v.shape), -1, axis)


WIDE = False


def mx_kscale(k):
    if not WIDE:
        return np.ones(k)
    levels = np.array([24, -24, 12, -12, 0])
    if k % 512:
        return np.exp2(np.random.permutation(np.resize(levels, k // 32))).repeat(32)
    a = np.empty((k // 512, 16))
    for p in range(k // 512):
        a[p, :8] = np.random.permutation(np.resize(levels, 8))
        for g in range(8):
            far = levels[np.abs(levels - a[p, g]) >= 10]
            a[p, g + 8] = far[np.random.randint(len(far))]
    return np.exp2(a.ravel()).repeat(32)


def f64(x):
    return np.asarray(x).astype(np.float64)


def striped(idx):
    return np.tile(idx.reshape(-1, 16).T, (8, 1)).astype(np.uint16)


def unstriped(offs):
    return offs[:16].T.reshape(-1).astype(np.int64)


E2M1 = np.array([0.0, 0.5, 1.0, 1.5, 2.0, 3.0, 4.0, 6.0, -0.0, -0.5, -1.0, -1.5, -2.0, -3.0, -4.0, -6.0])


def pack_weight(w, fmt):
    k, n = w.shape
    w = f64(np.asarray(w, np.float32).astype(ml_dtypes.bfloat16)).reshape(k // 32, 32, n)
    amax = np.abs(w).max(1)
    if fmt == "e4m3":
        byte = np.frexp(amax)[1] - 1 + 127 - 7
    else:
        mant, ex = np.frexp(amax / 6.0)
        byte = np.where(mant > 0.5, ex, ex - 1) + 127
    byte = np.clip(np.where(amax > 0, byte, 1), 1, 254)
    scaled = (w * np.exp2(127.0 - byte)[:, None, :]).reshape(k, n).astype(np.float32)
    by_word = np.ascontiguousarray(scaled.reshape(k // 512, 128, 4, n).transpose(0, 1, 3, 2))
    if fmt == "e4m3":
        words = by_word.astype(ml_dtypes.float8_e4m3fn).view(np.uint8)
    else:
        c = by_word.astype(ml_dtypes.float4_e2m1fn).view(np.uint8) & 0xF
        words = (c[..., 0::2] | (c[..., 1::2] << 4)).reshape(k // 512, 128, 2 * n)
    return np.ascontiguousarray(words), np.ascontiguousarray(byte.astype(np.uint8).reshape(k // 512, 16, n))


def unpack_weight(words, scales, fmt):
    g, _, n = scales.shape
    words = np.ascontiguousarray(words).reshape(g, 128, n, -1)
    if fmt == "e4m3":
        vals = words.view(ml_dtypes.float8_e4m3fn).astype(np.float64)
    else:
        nib = np.empty((g, 128, n, 4), np.uint8)
        nib[..., 0::2] = words & 0xF
        nib[..., 1::2] = words >> 4
        vals = E2M1[nib]
    vals = vals * np.repeat(np.exp2(scales.astype(np.float64) - 127.0), 8, axis=1)[..., None]
    return vals.transpose(0, 1, 3, 2).reshape(g * 512, n)


def pack_table4(v):
    words, scales = pack_weight(v, "e2m1")
    g, t = words.shape[0] // 2, v.shape[1]
    return np.ascontiguousarray(words.reshape(g, 2, 128, t, 2).transpose(0, 2, 3, 1, 4).reshape(g, 128, t, 4)), scales


def unpack_table4(words, scales):
    g, _, t, _ = words.shape
    return unpack_weight(words.reshape(g, 128, t, 2, 2).transpose(0, 3, 1, 2, 4).reshape(2 * g, 128, 2 * t), scales, "e2m1")


def gelu(f):
    return 0.5 * f * (1.0 + np.tanh(np.sqrt(2.0 / np.pi) * (f + 0.044715 * f**3)))


K, L, R, N, T, J = 1024, 512, 1024, 1024, 2048, 1024


def setup_inputs():
    n = np.random.standard_normal
    s = mx_kscale(K)[:, None]
    s2 = mx_kscale(L)[:, None]
    u = mx_kscale(R)[:, None]
    p_tab = pack_table4(n((K, T)) * s)
    p_tab2 = pack_weight(n((L, T)) * s2, "e4m3")
    p_wb = pack_weight(n((L, R)) / np.sqrt(L) / s2 * u.T, "e2m1")
    return {
        "tab_words": p_tab[0],
        "tab_scales": p_tab[1],
        "tab2_words": p_tab2[0],
        "tab2_scales": p_tab2[1],
        "wa": (n((K, R)) / np.sqrt(K) / s * u.T).astype(np.float32),
        "wb_words": p_wb[0],
        "wb_scales": p_wb[1],
        "en": (n((R, N)) / np.sqrt(R) / u).astype(np.float32),
        "b": (0.3 * n(N)).astype(np.float32),
        "offs": striped(np.random.permutation(T)[:J]),
        "offs2": striped(np.random.permutation(T)[:J]),
    }


def reference(tab_words, tab_scales, tab2_words, tab2_scales, wa, wb_words, wb_scales, en, b, offs, offs2):
    idx = unstriped(offs)
    idx2 = unstriped(offs2)
    tab_ = unpack_table4(tab_words, tab_scales)[:, idx]
    tab2_ = unpack_weight(tab2_words, tab2_scales, "e4m3")[:, idx2]
    wa_ = mxq(f64(wa), 0, "e4m3")
    wb_ = unpack_weight(wb_words, wb_scales, "e2m1")
    z = wa_.T @ tab_ + wb_.T @ tab2_
    h = np.maximum(z, 0.0)
    h_ = mxq(h, 0, "e4m3")
    en_ = mxq(f64(en), 0, "e4m3")
    y = en_.T @ h_
    return gelu(y + f64(b)[:, None])

@@ -1,0 +1,291 @@
+from contextlib import ExitStack
+
+import concourse.mybir as mybir
+
+K, L, R, N, T, J = 1024, 512, 1024, 1024, 2048, 1024
+FLOPS = 2 * J * R * (K + L) + 2 * J * R * N
+
+F32 = mybir.dt.float32
+BF16 = mybir.dt.bfloat16
+I32 = mybir.dt.int32
+U32 = mybir.dt.uint32
+U16 = mybir.dt.uint16
+U8 = mybir.dt.uint8
+FP8X4 = mybir.dt.float8_e4m3fn_x4
+FP4X4 = mybir.dt.float4_e2m1fn_x4
+ACT = mybir.ActivationFunctionType
+ALU = mybir.AluOpType
+
+P = 128
+PACK = 4
+KP = P * PACK
+HALF = 512
+CH = 128
+
+
+def tile_list_kg_relu_gelu_kernel(
+    tc, tab_words, tab_scales, tab2_words, tab2_scales, wa, wb_words, wb_scales, en, b, offs, offs2, out
+):
+    nc = tc.nc
+    with ExitStack() as ctx:
+        keep = ctx.enter_context(tc.tile_pool(name="keep", bufs=1))
+        arena = ctx.enter_context(tc.tile_pool(name="arena", bufs=1))
+        outs = ctx.enter_context(tc.tile_pool(name="outs", bufs=8))
+        psum = ctx.enter_context(tc.psum_pool(name="psum", bufs=1))
+
+        def held(name, width, dtype):
+            return keep.tile([P, width], dtype, name=name, align_bytes=64)
+
+        def placed(name, shape, dtype, offset):
+            return arena.tile(shape, dtype, name=name, align_bytes=64, offset=offset)
+
+        KB = 1024
+        list1 = keep.tile([P, J // 16], U16, name="list1")
+        list2 = keep.tile([P, J // 16], U16, name="list2")
+        tab_s = placed("tab_s", [P, T], U8, 16 * KB)
+        tab2_s = held("tab2_s", T, U8)
+        wb_w = held("wb_w", 2 * R, U8)
+        wb_s = held("wb_s", R, U8)
+        g1s_b = held("g1s_b", J, U8)
+        warm = placed("warm", [P, (11 * KB + 128) // 4], F32, 58 * KB - 64)
+        raw_at = {"wa00": 22 * KB, "wa01": 8 * KB + 512, "en10": 8 * KB + 768, "wa10": 50 * KB, "wa11": 50 * KB, "en11": 50 * KB,
+                  "en00": 32 * KB, "en01": 40 * KB}
+        grouped_at = {"wa00": 98 * KB, "wa10": 30 * KB, "wa01": 40 * KB, "wa11": 78 * KB, "en00": 82 * KB,
+                      "en10": 86 * KB, "en01": 90 * KB, "en11": 94 * KB}
+        scales_at = {"wa00": 16 * KB + 512, "hq00": 78 * KB, "hq01": 82 * KB, "hq10": 86 * KB, "hq11": 94 * KB}
+
+        def load_words(tile, src):
+            nc.sync.dma_start(out=tile[:].bitcast(I32), in_=src.bitcast(I32))
+
+        def load_rows(name, src, k0, c0):
+            raw = placed("raw_" + name, [P, PACK, HALF], F32, raw_at[name])
+            nc.sync.dma_start(out=raw[:], in_=src[k0 : k0 + KP, c0 : c0 + HALF].rearrange("(p j) w -> p j w", j=PACK))
+            return raw
+
+        def load_scales(engine, plane, src):
+            rows = 4 * src.shape[0]
+            for q in range(4):
+                engine.dma_start(
+                    out=plane[32 * q : 32 * q + rows, :].bitcast(I32),
+                    in_=src[:, 4 * q : 4 * q + 4, :].bitcast(I32),
+                )
+
+        raw = {}
+        nc.vector.memset(tab_s[:].bitcast(I32), 0)
+        nc.vector.memset(warm[:, 0:8], 0.0)
+        nc.gpsimd.memset(tab2_s[:].bitcast(I32), 0)
+        nc.sync.dma_start(list1[:], offs)
+        raw["wa00"] = load_rows("wa00", wa, 0, 0)
+        load_scales(nc.sync, tab_s, tab_scales)
+        nc.sync.dma_start(list2[:], offs2)
+        load_scales(nc.gpsimd, tab2_s, tab2_scales)
+        nc.gpsimd.memset(g1s_b[:].bitcast(I32), 0)
+        nc.scalar.activation(warm[:, 8:16], warm[:, 0:8], ACT.Gelu_apprx_tanh)
+        tab_w = placed("tab_w", [P, T], U32, 69 * KB)
+        load_words(tab_w, tab_words[0].rearrange("p t i -> p (t i)"))
+        raw["wa10"] = load_rows("wa10", wa, KP, 0)
+
+        def gather(picked, window, offsets):
+            nc.vector.tensor_copy(picked[:], window[:].indirect(offsets))
+            return picked
+
+        g1s_a = gather(held("g1s_a", J, U8), tab_s, list1[:])
+        nc.sync.dma_start(out=g1s_b[0:100, :].bitcast(I32), in_=g1s_a[4:104, :].bitcast(I32))
+        g1s = (g1s_a, g1s_b)
+
+        tab2_w = placed("tab2_w", [P, T], U32, 58 * KB)
+        wb_s_raw = placed("wb_s_raw", [P, R], U8, 68 * KB)
+        wb_w_raw = placed("wb_w_raw", [P, 2 * R], U8, 66 * KB)
+        load_words(tab2_w, tab2_words[0].rearrange("p t i -> p (t i)"))
+        load_words(wb_w_raw, wb_words[0])
+        nc.vector.memset(wb_s_raw[:].bitcast(I32), 0)
+        load_scales(nc.sync, wb_s_raw, wb_scales)
+
+        raw["wa01"] = load_rows("wa01", wa, 0, HALF)
+
+        def cast(on_scalar, dst, src):
+            if on_scalar:
+                nc.scalar.copy(dst, src)
+            else:
+                nc.vector.tensor_copy(dst, src)
+
+        def staging(name):
+            return placed("grouped_" + name, [P, PACK * HALF], BF16, grouped_at[name])
+
+        def round_wa(name, on_scalar):
+            grouped = staging(name)
+            cast(
+                on_scalar,
+                grouped[:].rearrange("p (t m j) -> p m j t", t=PACK, j=PACK),
+                raw[name][:].rearrange("p j (m t) -> p m j t", t=PACK),
+            )
+            return grouped[:]
+
+        def round_en(name, on_scalar):
+            grouped = staging(name)
+            cast(
+                on_scalar,
+                grouped[:].rearrange("p (c i j) -> p c j i", i=4, j=PACK),
+                raw[name][:].rearrange("p j (c i) -> p c j i", i=4),
+            )
+            return grouped[:]
+
+        def quantise(name, grouped):
+            codes = held(name + "_c", HALF, U32)
+            if name in scales_at:
+                scales = placed(name + "_s", [P, HALF], U8, scales_at[name])
+            else:
+                scales = held(name + "_s", HALF, U8)
+            nc.vector.quantize_mx(out=codes[:].bitcast(FP8X4), scales=scales[:], in_=grouped)
+            return codes, scales
+
+        QU = 256
+        g1w, g2w, g2s = {}, {}, {}
+        wa_q, en_q, h_q, banks = {}, {}, {}, {}
+
+        def gather_tab(u):
+            both = placed("both%d" % u, [P, QU * (3 if u == 0 else 1)], U32, (17, 17, 18, 19)[u] * KB + 512)
+            nc.vector.tensor_copy(both[:, 0:QU], tab_w[:].indirect(list1[:, 16 * u : 16 * u + 16]))
+            return both
+
+        def part_tab(u, both):
+            g1w[u] = placed("g1w0", [P, 4 * QU], U8, 98 * KB) if u == 0 else held("g1w%d" % u, 4 * QU, U8)
+            nc.vector.tensor_copy(
+                g1w[u][:].bitcast(U16).rearrange("p (d j) -> p d j", d=2),
+                both[:, 0:QU].bitcast(U16).rearrange("p (j d) -> p d j", d=2),
+            )
+
+        def deal_wb():
+            nc.vector.tensor_copy(
+                wb_w[:].bitcast(U16).rearrange("p (b t m) -> p b t m", b=2, t=PACK),
+                wb_w_raw[:].bitcast(U16).rearrange("p (b m t) -> p b t m", b=2, t=PACK),
+            )
+            nc.vector.tensor_copy(
+                wb_s[:].rearrange("p (b t m) -> p b t m", b=2, t=PACK),
+                wb_s_raw[:].rearrange("p (b m t) -> p b t m", b=2, t=PACK),
+            )
+
+        def open_bank(blk, c):
+            banks[blk, c] = psum.tile([P, PACK * CH], F32, name="bank%d" % c)
+
+        def pass_wb(blk, c, first, last):
+            jh, c4 = divmod(c, 4)
+            for t in range(PACK):
+                m0 = blk * HALF + t * P
+                nc.tensor.matmul_mx(
+                    out=banks[blk, c][:, t * CH : (t + 1) * CH],
+                    lhsT=wb_w[:, 2 * m0 : 2 * (m0 + P)].bitcast(FP4X4),
+                    lhsT_scale=wb_s[:, m0 : m0 + P],
+                    rhs=g2w[jh][:, c4 * CH : (c4 + 1) * CH].bitcast(FP8X4),
+                    rhs_scale=g2s[jh][:, c4 * CH : (c4 + 1) * CH],
+                    start=(first and t == 0),
+                    stop=(last and t == PACK - 1),
+                )
+
+        def pass_wa(a, blk, c, first, last):
+            codes, scales = wa_q[a, blk]
+            u, c2 = divmod(c, 2)
+            j0 = a * QU + c2 * CH
+            for t in range(PACK):
+                nc.tensor.matmul_mx(
+                    out=banks[blk, c][:, t * CH : (t + 1) * CH],
+                    lhsT=codes[:, t * P : (t + 1) * P].bitcast(FP8X4),
+                    lhsT_scale=scales[:, t * P : (t + 1) * P],
+                    rhs=g1w[u][:, 2 * j0 : 2 * (j0 + CH)].bitcast(FP4X4),
+                    rhs_scale=g1s[a][:, c * CH : (c + 1) * CH],
+                    start=(first and t == 0),
+                    stop=(last and t == PACK - 1),
+                )
+
+        h = {}
+
+        def relu_out(blk, c):
+            if c == 0 and blk == 0:
+                h[blk] = placed("h0", [P, PACK * J], BF16, 768)
+            elif c == 0:
+                h[blk] = held("h1", PACK * J, BF16)
+            nc.scalar.activation(
+                h[blk][:, c * KP : (c + 1) * KP].rearrange("p (j t) -> p j t", t=PACK),
+                banks[blk, c][:].rearrange("p (t j) -> p j t", t=PACK),
+                ACT.Relu,
+            )
+
+        def quantise_h(blk, jh):
+            h_q[blk, jh] = quantise("hq%d%d" % (blk, jh), h[blk][:, jh * 4 * KP : (jh + 1) * 4 * KP])
+
+        def score(nh, jh, first_bank):
+            for i in range(4):
+                nt = 4 * nh + i
+                bank = psum.tile([P, HALF], F32, name="bank%d" % (first_bank + i))
+                for blk in range(2):
+                    codes, scales = en_q[blk, nh]
+                    h_codes, h_scales = h_q[blk, jh]
+                    nc.tensor.matmul_mx(
+                        out=bank[:],
+                        lhsT=codes[:, i * P : (i + 1) * P].bitcast(FP8X4),
+                        lhsT_scale=scales[:, i * P : (i + 1) * P],
+                        rhs=h_codes[:].bitcast(FP8X4),
+                        rhs_scale=h_scales[:],
+                        start=(blk == 0),
+                        stop=(blk == 1),
+                    )
+                result = outs.tile([P, HALF], F32, name="result")
+                nc.scalar.activation(result[:], bank[:], ACT.Gelu_apprx_tanh, bias=bias[:, nt : nt + 1])
+                nc.sync.dma_start(out=out[nt * P : (nt + 1) * P, jh * HALF : (jh + 1) * HALF], in_=result[:])
+
+        grouped = round_wa("wa00", True)
+        for u in range(4):
+            both = gather_tab(u)
+            if u == 0:
+                wa_q[0, 0] = quantise("wa00", grouped)
+            part_tab(u, both)
+            for c in (2 * u, 2 * u + 1):
+                open_bank(0, c)
+                pass_wa(0, 0, c, True, False)
+        bias = placed("bias", [P, N // P], F32, 18 * KB + 512)
+        with nc.allow_non_contiguous_dma(reason="one bias value a partition"):
+            nc.sync.dma_start(out=bias[:], in_=b.rearrange("(c p) -> p c", p=P))
+        g2s[0] = gather(placed("g2s0", [P, HALF], U8, 19 * KB + 512), tab2_s, list2[:, 0:32])
+        grouped = round_wa("wa10", True)
+        raw["wa11"] = load_rows("wa11", wa, KP, HALF)
+        wa_q[1, 0] = quantise("wa10", grouped)
+        raw["en00"] = load_rows("en00", en, 0, 0)
+        for c in range(8):
+            pass_wa(1, 0, c, False, False)
+        g2w[0] = gather(placed("g2w0", [P, HALF], U32, 30 * KB), tab2_w, list2[:, 0:32])
+        deal_wb()
+        grouped = round_wa("wa01", True)
+        raw["en10"] = load_rows("en10", en, KP, 0)
+        for c in range(4):
+            pass_wb(0, c, False, True)
+            relu_out(0, c)
+        g2s[1] = gather(placed("g2s1", [P, HALF], U8, 68 * KB), tab2_s, list2[:, 32:64])
+        g2w[1] = gather(placed("g2w1", [P, HALF], U32, 66 * KB), tab2_w, list2[:, 32:64])
+        for c in range(4, 8):
+            pass_wb(0, c, False, True)
+            relu_out(0, c)
+        wa_q[0, 1] = quantise("wa01", grouped)
+        raw["en01"] = load_rows("en01", en, 0, HALF)
+        grouped = round_wa("wa11", False)
+        raw["en11"] = load_rows("en11", en, KP, HALF)
+        wa_q[1, 1] = quantise("wa11", grouped)
+        quantise_h(0, 0)
+        for jh in range(2):
+            cs = range(4 * jh, 4 * jh + 4)
+            for c in cs:
+                open_bank(1, c)
+                pass_wb(1, c, True, False)
+            for c in cs:
+                pass_wa(0, 1, c, False, False)
+            for c in cs:
+                pass_wa(1, 1, c, False, True)
+                relu_out(1, c)
+            en_q[jh, 0] = quantise("en%d0" % jh, round_en("en%d0" % jh, False))
+            quantise_h(jh, 1 - jh)
+        score(0, 0, 4)
+        for blk in range(2):
+            en_q[blk, 1] = quantise("en%d1" % blk, round_en("en%d1" % blk, False))
+        quantise_h(1, 1)
+        score(1, 0, 0)
+        score(0, 1, 4)
+        score(1, 1, 0)

@@ -1,6 +1,7 @@
 from contextlib import ExitStack
 
 import concourse.mybir as mybir
+from concourse.masks import make_identity
 
 K, L, R, N, T, J = 1024, 512, 1024, 1024, 2048, 1024
 FLOPS = 2 * J * R * (K + L) + 2 * J * R * N
@@ -48,9 +49,9 @@ def tile_list_kg_relu_gelu_kernel(
         wb_s = held("wb_s", R, U8)
         g1s_b = held("g1s_b", J, U8)
         warm = placed("warm", [P, (11 * KB + 128) // 4], F32, 58 * KB - 64)
-        raw_at = {"wa00": 22 * KB, "wa01": 8 * KB + 512, "en10": 8 * KB + 768, "wa10": 50 * KB, "wa11": 50 * KB, "en11": 50 * KB,
-                  "en00": 32 * KB, "en01": 40 * KB}
-        grouped_at = {"wa00": 98 * KB, "wa10": 30 * KB, "wa01": 40 * KB, "wa11": 78 * KB, "en00": 82 * KB,
+        raw_at = {"wa00": 22 * KB, "wa01": 8 * KB + 512, "en10": 22 * KB + 256, "wa10": 50 * KB, "wa11": 50 * KB, "en11": 50 * KB,
+                  "en00": 32 * KB + 256, "en01": 41 * KB}
+        grouped_at = {"wa00": 98 * KB, "wa10": 30 * KB, "wa01": 41 * KB, "wa11": 78 * KB, "en00": 82 * KB,
                       "en10": 86 * KB, "en01": 90 * KB, "en11": 94 * KB}
         scales_at = {"wa00": 16 * KB + 512, "hq00": 78 * KB, "hq01": 82 * KB, "hq10": 86 * KB, "hq11": 94 * KB}
 
@@ -60,6 +61,13 @@ def tile_list_kg_relu_gelu_kernel(
         def load_rows(name, src, k0, c0):
             raw = placed("raw_" + name, [P, PACK, HALF], F32, raw_at[name])
             nc.sync.dma_start(out=raw[:], in_=src[k0 : k0 + KP, c0 : c0 + HALF].rearrange("(p j) w -> p j w", j=PACK))
+            return raw
+
+        def load_en(name, blk, nh):
+            raw = placed("raw_" + name, [P, PACK, HALF], F32, raw_at[name])
+            rows = en[blk * KP : (blk + 1) * KP, nh * HALF : (nh + 1) * HALF].rearrange("(g t i) n -> t g i n", t=PACK, i=4)
+            for t in range(PACK):
+                nc.sync.dma_start(out=raw[:, t, :], in_=rows[t])
             return raw
 
         def load_scales(engine, plane, src):
@@ -80,6 +88,12 @@ def tile_list_kg_relu_gelu_kernel(
         nc.sync.dma_start(list2[:], offs2)
         load_scales(nc.gpsimd, tab2_s, tab2_scales)
         nc.gpsimd.memset(g1s_b[:].bitcast(I32), 0)
+        bias_rows = held("bias_rows", P, F32)
+        identity = held("identity", P, F32)
+        bias = held("bias", N // P, F32)
+        nc.gpsimd.memset(bias_rows[:], 0.0)
+        nc.gpsimd.dma_start(out=bias_rows[0 : N // P, :], in_=b.rearrange("(c p) -> c p", p=P))
+        make_identity(nc, identity[:])
         nc.scalar.activation(warm[:, 8:16], warm[:, 0:8], ACT.Gelu_apprx_tanh)
         tab_w = placed("tab_w", [P, T], U32, 69 * KB)
         load_words(tab_w, tab_words[0].rearrange("p t i -> p (t i)"))
@@ -116,8 +130,8 @@ def tile_list_kg_relu_gelu_kernel(
             grouped = staging(name)
             cast(
                 on_scalar,
-                grouped[:].rearrange("p (t m j) -> p m j t", t=PACK, j=PACK),
-                raw[name][:].rearrange("p j (m t) -> p m j t", t=PACK),
+                grouped[:].rearrange("p (t g i j) -> p g t j i", t=PACK, i=4, j=PACK),
+                raw[name][:].rearrange("p j (g t i) -> p g t j i", t=PACK, i=4),
             )
             return grouped[:]
 
@@ -157,12 +171,12 @@ def tile_list_kg_relu_gelu_kernel(
 
         def deal_wb():
             nc.vector.tensor_copy(
-                wb_w[:].bitcast(U16).rearrange("p (b t m) -> p b t m", b=2, t=PACK),
-                wb_w_raw[:].bitcast(U16).rearrange("p (b m t) -> p b t m", b=2, t=PACK),
+                wb_w[:].bitcast(I32).rearrange("p (b t g w) -> p b t g w", b=2, t=PACK, w=2),
+                wb_w_raw[:].bitcast(I32).rearrange("p (b g t w) -> p b t g w", b=2, t=PACK, w=2),
             )
             nc.vector.tensor_copy(
-                wb_s[:].rearrange("p (b t m) -> p b t m", b=2, t=PACK),
-                wb_s_raw[:].rearrange("p (b m t) -> p b t m", b=2, t=PACK),
+                wb_s[:].bitcast(I32).rearrange("p (b t g) -> p b t g", b=2, t=PACK),
+                wb_s_raw[:].bitcast(I32).rearrange("p (b g t) -> p b t g", b=2, t=PACK),
             )
 
         def open_bank(blk, c):
@@ -213,10 +227,10 @@ def tile_list_kg_relu_gelu_kernel(
         def quantise_h(blk, jh):
             h_q[blk, jh] = quantise("hq%d%d" % (blk, jh), h[blk][:, jh * 4 * KP : (jh + 1) * 4 * KP])
 
-        def score(nh, jh, first_bank):
+        def score(nh, jh, bank_ids):
             for i in range(4):
                 nt = 4 * nh + i
-                bank = psum.tile([P, HALF], F32, name="bank%d" % (first_bank + i))
+                bank = psum.tile([P, HALF], F32, name="bank%d" % bank_ids[i])
                 for blk in range(2):
                     codes, scales = en_q[blk, nh]
                     h_codes, h_scales = h_q[blk, jh]
@@ -242,20 +256,17 @@ def tile_list_kg_relu_gelu_kernel(
             for c in (2 * u, 2 * u + 1):
                 open_bank(0, c)
                 pass_wa(0, 0, c, True, False)
-        bias = placed("bias", [P, N // P], F32, 18 * KB + 512)
-        with nc.allow_non_contiguous_dma(reason="one bias value a partition"):
-            nc.sync.dma_start(out=bias[:], in_=b.rearrange("(c p) -> p c", p=P))
         g2s[0] = gather(placed("g2s0", [P, HALF], U8, 19 * KB + 512), tab2_s, list2[:, 0:32])
         grouped = round_wa("wa10", True)
         raw["wa11"] = load_rows("wa11", wa, KP, HALF)
         wa_q[1, 0] = quantise("wa10", grouped)
-        raw["en00"] = load_rows("en00", en, 0, 0)
+        raw["en00"] = load_en("en00", 0, 0)
+        raw["en10"] = load_en("en10", 1, 0)
         for c in range(8):
             pass_wa(1, 0, c, False, False)
-        g2w[0] = gather(placed("g2w0", [P, HALF], U32, 30 * KB), tab2_w, list2[:, 0:32])
+        g2w[0] = gather(placed("g2w0", [P, HALF], U32, 30 * KB + 256), tab2_w, list2[:, 0:32])
         deal_wb()
         grouped = round_wa("wa01", True)
-        raw["en10"] = load_rows("en10", en, KP, 0)
         for c in range(4):
             pass_wb(0, c, False, True)
             relu_out(0, c)
@@ -265,13 +276,13 @@ def tile_list_kg_relu_gelu_kernel(
             pass_wb(0, c, False, True)
             relu_out(0, c)
         wa_q[0, 1] = quantise("wa01", grouped)
-        raw["en01"] = load_rows("en01", en, 0, HALF)
+        raw["en01"] = load_en("en01", 0, 1)
         grouped = round_wa("wa11", False)
-        raw["en11"] = load_rows("en11", en, KP, HALF)
+        raw["en11"] = load_en("en11", 1, 1)
         wa_q[1, 1] = quantise("wa11", grouped)
         quantise_h(0, 0)
-        for jh in range(2):
-            cs = range(4 * jh, 4 * jh + 4)
+
+        def project_upper(cs):
             for c in cs:
                 open_bank(1, c)
                 pass_wb(1, c, True, False)
@@ -280,12 +291,20 @@ def tile_list_kg_relu_gelu_kernel(
             for c in cs:
                 pass_wa(1, 1, c, False, True)
                 relu_out(1, c)
-            en_q[jh, 0] = quantise("en%d0" % jh, round_en("en%d0" % jh, False))
-            quantise_h(jh, 1 - jh)
-        score(0, 0, 4)
+
+        turned = psum.tile([P, P], F32, name="bank7")
+        nc.tensor.transpose(turned[:], bias_rows[:], identity[:])
+        nc.scalar.copy(bias[:], turned[:, 0 : N // P])
+        project_upper(range(0, 4))
+        for blk in range(2):
+            en_q[blk, 0] = quantise("en%d0" % blk, round_en("en%d0" % blk, False))
+            quantise_h(blk, 1 - blk)
+        project_upper(range(4, 6))
+        score(0, 0, (6, 7, 0, 1))
+        project_upper(range(6, 8))
         for blk in range(2):
             en_q[blk, 1] = quantise("en%d1" % blk, round_en("en%d1" % blk, False))
         quantise_h(1, 1)
-        score(1, 0, 0)
-        score(0, 1, 4)
-        score(1, 1, 0)
+        score(1, 0, (2, 3, 0, 1))
+        score(0, 1, (4, 5, 2, 3))
+        score(1, 1, (6, 7, 0, 1))

@@ -52,8 +52,8 @@ def tile_list_kg_relu_gelu_kernel(
         raw_at = {"wa00": 22 * KB, "wa01": 8 * KB + 512, "en10": 22 * KB + 256, "wa10": 50 * KB, "wa11": 50 * KB, "en11": 50 * KB,
                   "en00": 32 * KB + 256, "en01": 41 * KB}
         grouped_at = {"wa00": 98 * KB, "wa10": 30 * KB, "wa01": 41 * KB, "wa11": 78 * KB, "en00": 82 * KB,
-                      "en10": 86 * KB, "en01": 90 * KB, "en11": 94 * KB}
-        scales_at = {"wa00": 16 * KB + 512, "hq00": 78 * KB, "hq01": 82 * KB, "hq10": 86 * KB, "hq11": 94 * KB}
+                      "en10": 86 * KB, "en01": 90 * KB, "en11": 106 * KB}
+        scales_at = {"wa00": 16 * KB + 512, "hq00": 33 * KB, "hq01": 23 * KB, "hq10": 86 * KB, "hq11": 50 * KB}
 
         def load_words(tile, src):
             nc.sync.dma_start(out=tile[:].bitcast(I32), in_=src.bitcast(I32))
@@ -243,9 +243,14 @@ def tile_list_kg_relu_gelu_kernel(
                         start=(blk == 0),
                         stop=(blk == 1),
                     )
-                result = outs.tile([P, HALF], F32, name="result")
-                nc.scalar.activation(result[:], bank[:], ACT.Gelu_apprx_tanh, bias=bias[:, nt : nt + 1])
-                nc.sync.dma_start(out=out[nt * P : (nt + 1) * P, jh * HALF : (jh + 1) * HALF], in_=result[:])
+                width = HALF // 2 if (nh, jh, i) == (1, 1, 3) else HALF
+                for j0 in range(0, HALF, width):
+                    result = outs.tile([P, width], F32, name="result")
+                    nc.scalar.activation(
+                        result[:], bank[:, j0 : j0 + width], ACT.Gelu_apprx_tanh, bias=bias[:, nt : nt + 1]
+                    )
+                    col = jh * HALF + j0
+                    nc.sync.dma_start(out=out[nt * P : (nt + 1) * P, col : col + width], in_=result[:])
 
         grouped = round_wa("wa00", True)
         for u in range(4):
@@ -280,15 +285,12 @@ def tile_list_kg_relu_gelu_kernel(
         grouped = round_wa("wa11", False)
         raw["en11"] = load_en("en11", 1, 1)
         wa_q[1, 1] = quantise("wa11", grouped)
-        quantise_h(0, 0)
 
         def project_upper(cs):
             for c in cs:
                 open_bank(1, c)
                 pass_wb(1, c, True, False)
-            for c in cs:
                 pass_wa(0, 1, c, False, False)
-            for c in cs:
                 pass_wa(1, 1, c, False, True)
                 relu_out(1, c)
 
@@ -297,14 +299,16 @@ def tile_list_kg_relu_gelu_kernel(
         nc.scalar.copy(bias[:], turned[:, 0 : N // P])
         project_upper(range(0, 4))
         for blk in range(2):
-            en_q[blk, 0] = quantise("en%d0" % blk, round_en("en%d0" % blk, False))
-            quantise_h(blk, 1 - blk)
-        project_upper(range(4, 6))
-        score(0, 0, (6, 7, 0, 1))
-        project_upper(range(6, 8))
-        for blk in range(2):
-            en_q[blk, 1] = quantise("en%d1" % blk, round_en("en%d1" % blk, False))
+            grouped = round_en("en%d0" % blk, False)
+            quantise_h(0, blk)
+            en_q[blk, 0] = quantise("en%d0" % blk, grouped)
+        quantise_h(1, 0)
+        project_upper(range(4, 8))
+        en_q[0, 1] = quantise("en01", round_en("en01", False))
+        grouped = round_en("en11", False)
         quantise_h(1, 1)
-        score(1, 0, (2, 3, 0, 1))
-        score(0, 1, (4, 5, 2, 3))
-        score(1, 1, (6, 7, 0, 1))
+        score(0, 0, (0, 1, 2, 3))
+        en_q[1, 1] = quantise("en11", grouped)
+        score(0, 1, (4, 5, 6, 7))
+        score(1, 0, (0, 1, 2, 3))
+        score(1, 1, (4, 5, 6, 7))

@@ -43,13 +43,13 @@ def tile_list_kg_relu_gelu_kernel(
         KB = 1024
         list1 = keep.tile([P, J // 16], U16, name="list1")
         list2 = keep.tile([P, J // 16], U16, name="list2")
-        tab_s = placed("tab_s", [P, T], U8, 16 * KB)
+        tab_s = placed("tab_s", [P, 3 * T], U8, 16 * KB)
         tab2_s = held("tab2_s", T, U8)
         wb_w = held("wb_w", 2 * R, U8)
         wb_s = held("wb_s", R, U8)
         g1s_b = held("g1s_b", J, U8)
         warm = placed("warm", [P, (11 * KB + 128) // 4], F32, 58 * KB - 64)
-        raw_at = {"wa00": 22 * KB, "wa01": 8 * KB + 512, "en10": 22 * KB + 256, "wa10": 50 * KB, "wa11": 50 * KB, "en11": 50 * KB,
+        raw_at = {"wa00": 69 * KB, "wa01": 8 * KB + 512, "en10": 22 * KB + 256, "wa10": 50 * KB, "wa11": 50 * KB, "en11": 50 * KB,
                   "en00": 32 * KB + 256, "en01": 41 * KB}
         grouped_at = {"wa00": 98 * KB, "wa10": 30 * KB, "wa01": 41 * KB, "wa11": 78 * KB, "en00": 82 * KB,
                       "en10": 86 * KB, "en01": 90 * KB, "en11": 106 * KB}
@@ -79,12 +79,13 @@ def tile_list_kg_relu_gelu_kernel(
                 )
 
         raw = {}
-        nc.vector.memset(tab_s[:].bitcast(I32), 0)
+        nc.vector.memset(tab_s[:, 0:T].bitcast(I32), 0)
         nc.vector.memset(warm[:, 0:8], 0.0)
         nc.gpsimd.memset(tab2_s[:].bitcast(I32), 0)
         nc.sync.dma_start(list1[:], offs)
-        raw["wa00"] = load_rows("wa00", wa, 0, 0)
-        load_scales(nc.sync, tab_s, tab_scales)
+        tab_w = placed("tab_w", [P, T], U32, 22 * KB)
+        load_words(tab_w, tab_words[0].rearrange("p t i -> p (t i)"))
+        load_scales(nc.sync, tab_s[:, 0:T], tab_scales)
         nc.sync.dma_start(list2[:], offs2)
         load_scales(nc.gpsimd, tab2_s, tab2_scales)
         nc.gpsimd.memset(g1s_b[:].bitcast(I32), 0)
@@ -95,15 +96,14 @@ def tile_list_kg_relu_gelu_kernel(
         nc.gpsimd.dma_start(out=bias_rows[0 : N // P, :], in_=b.rearrange("(c p) -> c p", p=P))
         make_identity(nc, identity[:])
         nc.scalar.activation(warm[:, 8:16], warm[:, 0:8], ACT.Gelu_apprx_tanh)
-        tab_w = placed("tab_w", [P, T], U32, 69 * KB)
-        load_words(tab_w, tab_words[0].rearrange("p t i -> p (t i)"))
+        raw["wa00"] = load_rows("wa00", wa, 0, 0)
         raw["wa10"] = load_rows("wa10", wa, KP, 0)
 
         def gather(picked, window, offsets):
-            nc.vector.tensor_copy(picked[:], window[:].indirect(offsets))
+            nc.vector.tensor_copy(picked[:], window.indirect(offsets))
             return picked
 
-        g1s_a = gather(held("g1s_a", J, U8), tab_s, list1[:])
+        g1s_a = gather(held("g1s_a", J, U8), tab_s[:, 0:T], list1[:])
         nc.sync.dma_start(out=g1s_b[0:100, :].bitcast(I32), in_=g1s_a[4:104, :].bitcast(I32))
         g1s = (g1s_a, g1s_b)
 
@@ -158,12 +158,12 @@ def tile_list_kg_relu_gelu_kernel(
         wa_q, en_q, h_q, banks = {}, {}, {}, {}
 
         def gather_tab(u):
-            both = placed("both%d" % u, [P, QU * (3 if u == 0 else 1)], U32, (17, 17, 18, 19)[u] * KB + 512)
+            both = placed("both%d" % u, [P, QU], U32, (102, 18, 19, 98)[u] * KB)
             nc.vector.tensor_copy(both[:, 0:QU], tab_w[:].indirect(list1[:, 16 * u : 16 * u + 16]))
             return both
 
         def part_tab(u, both):
-            g1w[u] = placed("g1w0", [P, 4 * QU], U8, 98 * KB) if u == 0 else held("g1w%d" % u, 4 * QU, U8)
+            g1w[u] = held("g1w%d" % u, 4 * QU, U8)
             nc.vector.tensor_copy(
                 g1w[u][:].bitcast(U16).rearrange("p (d j) -> p d j", d=2),
                 both[:, 0:QU].bitcast(U16).rearrange("p (j d) -> p d j", d=2),
@@ -253,15 +253,13 @@ def tile_list_kg_relu_gelu_kernel(
                     nc.sync.dma_start(out=out[nt * P : (nt + 1) * P, col : col + width], in_=result[:])
 
         grouped = round_wa("wa00", True)
+        wa_q[0, 0] = quantise("wa00", grouped)
         for u in range(4):
-            both = gather_tab(u)
-            if u == 0:
-                wa_q[0, 0] = quantise("wa00", grouped)
-            part_tab(u, both)
+            part_tab(u, gather_tab(u))
             for c in (2 * u, 2 * u + 1):
                 open_bank(0, c)
                 pass_wa(0, 0, c, True, False)
-        g2s[0] = gather(placed("g2s0", [P, HALF], U8, 19 * KB + 512), tab2_s, list2[:, 0:32])
+        g2s[0] = gather(placed("g2s0", [P, HALF], U8, 98 * KB), tab2_s[:], list2[:, 0:32])
         grouped = round_wa("wa10", True)
         raw["wa11"] = load_rows("wa11", wa, KP, HALF)
         wa_q[1, 0] = quantise("wa10", grouped)
@@ -269,14 +267,14 @@ def tile_list_kg_relu_gelu_kernel(
         raw["en10"] = load_en("en10", 1, 0)
         for c in range(8):
             pass_wa(1, 0, c, False, False)
-        g2w[0] = gather(placed("g2w0", [P, HALF], U32, 30 * KB + 256), tab2_w, list2[:, 0:32])
+        g2w[0] = gather(placed("g2w0", [P, HALF], U32, 30 * KB + 256), tab2_w[:], list2[:, 0:32])
         deal_wb()
         grouped = round_wa("wa01", True)
         for c in range(4):
             pass_wb(0, c, False, True)
             relu_out(0, c)
-        g2s[1] = gather(placed("g2s1", [P, HALF], U8, 68 * KB), tab2_s, list2[:, 32:64])
-        g2w[1] = gather(placed("g2w1", [P, HALF], U32, 66 * KB), tab2_w, list2[:, 32:64])
+        g2s[1] = gather(placed("g2s1", [P, HALF], U8, 68 * KB), tab2_s[:], list2[:, 32:64])
+        g2w[1] = gather(placed("g2w1", [P, HALF], U32, 66 * KB), tab2_w[:], list2[:, 32:64])
         for c in range(4, 8):
             pass_wb(0, c, False, True)
             relu_out(0, c)

from contextlib import ExitStack

import concourse.mybir as mybir
from concourse.masks import make_identity

K, L, R, N, T, J = 1024, 512, 1024, 1024, 2048, 1024
FLOPS = 2 * J * R * (K + L) + 2 * J * R * N

F32 = mybir.dt.float32
BF16 = mybir.dt.bfloat16
I32 = mybir.dt.int32
U32 = mybir.dt.uint32
U16 = mybir.dt.uint16
U8 = mybir.dt.uint8
FP8X4 = mybir.dt.float8_e4m3fn_x4
FP4X4 = mybir.dt.float4_e2m1fn_x4
ACT = mybir.ActivationFunctionType
ALU = mybir.AluOpType

P = 128
PACK = 4
KP = P * PACK
HALF = 512
CH = 128


def tile_list_kg_relu_gelu_kernel(
    tc, tab_words, tab_scales, tab2_words, tab2_scales, wa, wb_words, wb_scales, en, b, offs, offs2, out
):
    nc = tc.nc
    with ExitStack() as ctx:
        keep = ctx.enter_context(tc.tile_pool(name="keep", bufs=1))
        arena = ctx.enter_context(tc.tile_pool(name="arena", bufs=1))
        outs = ctx.enter_context(tc.tile_pool(name="outs", bufs=8))
        psum = ctx.enter_context(tc.psum_pool(name="psum", bufs=1))

        def held(name, width, dtype):
            return keep.tile([P, width], dtype, name=name, align_bytes=64)

        def placed(name, shape, dtype, offset):
            return arena.tile(shape, dtype, name=name, align_bytes=64, offset=offset)

        KB = 1024
        list1 = keep.tile([P, J // 16], U16, name="list1")
        list2 = keep.tile([P, J // 16], U16, name="list2")
        tab_s = placed("tab_s", [P, 3 * T], U8, 16 * KB)
        tab2_s = held("tab2_s", T, U8)
        wb_w = held("wb_w", 2 * R, U8)
        wb_s = held("wb_s", R, U8)
        g1s_b = held("g1s_b", J, U8)
        warm = placed("warm", [P, (11 * KB + 128) // 4], F32, 58 * KB - 64)
        raw_at = {"wa00": 69 * KB, "wa01": 8 * KB + 512, "en10": 22 * KB + 256, "wa10": 50 * KB, "wa11": 50 * KB, "en11": 50 * KB,
                  "en00": 32 * KB + 256, "en01": 41 * KB}
        grouped_at = {"wa00": 98 * KB, "wa10": 30 * KB, "wa01": 41 * KB, "wa11": 78 * KB, "en00": 82 * KB,
                      "en10": 86 * KB, "en01": 90 * KB, "en11": 106 * KB}
        scales_at = {"wa00": 16 * KB + 512, "hq00": 33 * KB, "hq01": 23 * KB, "hq10": 86 * KB, "hq11": 50 * KB}

        def load_words(tile, src):
            nc.sync.dma_start(out=tile[:].bitcast(I32), in_=src.bitcast(I32))

        def load_rows(name, src, k0, c0):
            raw = placed("raw_" + name, [P, PACK, HALF], F32, raw_at[name])
            nc.sync.dma_start(out=raw[:], in_=src[k0 : k0 + KP, c0 : c0 + HALF].rearrange("(p j) w -> p j w", j=PACK))
            return raw

        def load_en(name, blk, nh):
            raw = placed("raw_" + name, [P, PACK, HALF], F32, raw_at[name])
            rows = en[blk * KP : (blk + 1) * KP, nh * HALF : (nh + 1) * HALF].rearrange("(g t i) n -> t g i n", t=PACK, i=4)
            for t in range(PACK):
                nc.sync.dma_start(out=raw[:, t, :], in_=rows[t])
            return raw

        def load_scales(engine, plane, src):
            rows = 4 * src.shape[0]
            for q in range(4):
                engine.dma_start(
                    out=plane[32 * q : 32 * q + rows, :].bitcast(I32),
                    in_=src[:, 4 * q : 4 * q + 4, :].bitcast(I32),
                )

        raw = {}
        nc.vector.memset(tab_s[:, 0:T].bitcast(I32), 0)
        nc.vector.memset(warm[:, 0:8], 0.0)
        nc.gpsimd.memset(tab2_s[:].bitcast(I32), 0)
        nc.sync.dma_start(list1[:], offs)
        tab_w = placed("tab_w", [P, T], U32, 22 * KB)
        load_words(tab_w, tab_words[0].rearrange("p t i -> p (t i)"))
        load_scales(nc.sync, tab_s[:, 0:T], tab_scales)
        nc.sync.dma_start(list2[:], offs2)
        load_scales(nc.gpsimd, tab2_s, tab2_scales)
        nc.gpsimd.memset(g1s_b[:].bitcast(I32), 0)
        bias_rows = held("bias_rows", P, F32)
        identity = held("identity", P, F32)
        bias = held("bias", N // P, F32)
        nc.gpsimd.memset(bias_rows[:], 0.0)
        nc.gpsimd.dma_start(out=bias_rows[0 : N // P, :], in_=b.rearrange("(c p) -> c p", p=P))
        make_identity(nc, identity[:])
        nc.scalar.activation(warm[:, 8:16], warm[:, 0:8], ACT.Gelu_apprx_tanh)
        raw["wa00"] = load_rows("wa00", wa, 0, 0)
        raw["wa10"] = load_rows("wa10", wa, KP, 0)

        def gather(picked, window, offsets):
            nc.vector.tensor_copy(picked[:], window.indirect(offsets))
            return picked

        g1s_a = gather(held("g1s_a", J, U8), tab_s[:, 0:T], list1[:])
        nc.sync.dma_start(out=g1s_b[0:100, :].bitcast(I32), in_=g1s_a[4:104, :].bitcast(I32))
        g1s = (g1s_a, g1s_b)

        tab2_w = placed("tab2_w", [P, T], U32, 58 * KB)
        wb_s_raw = placed("wb_s_raw", [P, R], U8, 68 * KB)
        wb_w_raw = placed("wb_w_raw", [P, 2 * R], U8, 66 * KB)
        load_words(tab2_w, tab2_words[0].rearrange("p t i -> p (t i)"))
        load_words(wb_w_raw, wb_words[0])
        nc.vector.memset(wb_s_raw[:].bitcast(I32), 0)
        load_scales(nc.sync, wb_s_raw, wb_scales)

        raw["wa01"] = load_rows("wa01", wa, 0, HALF)

        def cast(on_scalar, dst, src):
            if on_scalar:
                nc.scalar.copy(dst, src)
            else:
                nc.vector.tensor_copy(dst, src)

        def staging(name):
            return placed("grouped_" + name, [P, PACK * HALF], BF16, grouped_at[name])

        def round_wa(name, on_scalar):
            grouped = staging(name)
            cast(
                on_scalar,
                grouped[:].rearrange("p (t g i j) -> p g t j i", t=PACK, i=4, j=PACK),
                raw[name][:].rearrange("p j (g t i) -> p g t j i", t=PACK, i=4),
            )
            return grouped[:]

        def round_en(name, on_scalar):
            grouped = staging(name)
            cast(
                on_scalar,
                grouped[:].rearrange("p (c i j) -> p c j i", i=4, j=PACK),
                raw[name][:].rearrange("p j (c i) -> p c j i", i=4),
            )
            return grouped[:]

        def quantise(name, grouped):
            codes = held(name + "_c", HALF, U32)
            if name in scales_at:
                scales = placed(name + "_s", [P, HALF], U8, scales_at[name])
            else:
                scales = held(name + "_s", HALF, U8)
            nc.vector.quantize_mx(out=codes[:].bitcast(FP8X4), scales=scales[:], in_=grouped)
            return codes, scales

        QU = 256
        g1w, g2w, g2s = {}, {}, {}
        wa_q, en_q, h_q, banks = {}, {}, {}, {}

        def gather_tab(u):
            both = placed("both%d" % u, [P, QU], U32, (102, 18, 19, 98)[u] * KB)
            nc.vector.tensor_copy(both[:, 0:QU], tab_w[:].indirect(list1[:, 16 * u : 16 * u + 16]))
            return both

        def part_tab(u, both):
            g1w[u] = held("g1w%d" % u, 4 * QU, U8)
            nc.vector.tensor_copy(
                g1w[u][:].bitcast(U16).rearrange("p (d j) -> p d j", d=2),
                both[:, 0:QU].bitcast(U16).rearrange("p (j d) -> p d j", d=2),
            )

        def deal_wb():
            nc.vector.tensor_copy(
                wb_w[:].bitcast(I32).rearrange("p (b t g w) -> p b t g w", b=2, t=PACK, w=2),
                wb_w_raw[:].bitcast(I32).rearrange("p (b g t w) -> p b t g w", b=2, t=PACK, w=2),
            )
            nc.vector.tensor_copy(
                wb_s[:].bitcast(I32).rearrange("p (b t g) -> p b t g", b=2, t=PACK),
                wb_s_raw[:].bitcast(I32).rearrange("p (b g t) -> p b t g", b=2, t=PACK),
            )

        def open_bank(blk, c):
            banks[blk, c] = psum.tile([P, PACK * CH], F32, name="bank%d" % c)

        def pass_wb(blk, c, first, last):
            jh, c4 = divmod(c, 4)
            for t in range(PACK):
                m0 = blk * HALF + t * P
                nc.tensor.matmul_mx(
                    out=banks[blk, c][:, t * CH : (t + 1) * CH],
                    lhsT=wb_w[:, 2 * m0 : 2 * (m0 + P)].bitcast(FP4X4),
                    lhsT_scale=wb_s[:, m0 : m0 + P],
                    rhs=g2w[jh][:, c4 * CH : (c4 + 1) * CH].bitcast(FP8X4),
                    rhs_scale=g2s[jh][:, c4 * CH : (c4 + 1) * CH],
                    start=(first and t == 0),
                    stop=(last and t == PACK - 1),
                )

        def pass_wa(a, blk, c, first, last):
            codes, scales = wa_q[a, blk]
            u, c2 = divmod(c, 2)
            j0 = a * QU + c2 * CH
            for t in range(PACK):
                nc.tensor.matmul_mx(
                    out=banks[blk, c][:, t * CH : (t + 1) * CH],
                    lhsT=codes[:, t * P : (t + 1) * P].bitcast(FP8X4),
                    lhsT_scale=scales[:, t * P : (t + 1) * P],
                    rhs=g1w[u][:, 2 * j0 : 2 * (j0 + CH)].bitcast(FP4X4),
                    rhs_scale=g1s[a][:, c * CH : (c + 1) * CH],
                    start=(first and t == 0),
                    stop=(last and t == PACK - 1),
                )

        h = {}

        def relu_out(blk, c):
            if c == 0 and blk == 0:
                h[blk] = placed("h0", [P, PACK * J], BF16, 768)
            elif c == 0:
                h[blk] = held("h1", PACK * J, BF16)
            nc.scalar.activation(
                h[blk][:, c * KP : (c + 1) * KP].rearrange("p (j t) -> p j t", t=PACK),
                banks[blk, c][:].rearrange("p (t j) -> p j t", t=PACK),
                ACT.Relu,
            )

        def quantise_h(blk, jh):
            h_q[blk, jh] = quantise("hq%d%d" % (blk, jh), h[blk][:, jh * 4 * KP : (jh + 1) * 4 * KP])

        def score(nh, jh, bank_ids):
            for i in range(4):
                nt = 4 * nh + i
                bank = psum.tile([P, HALF], F32, name="bank%d" % bank_ids[i])
                for blk in range(2):
                    codes, scales = en_q[blk, nh]
                    h_codes, h_scales = h_q[blk, jh]
                    nc.tensor.matmul_mx(
                        out=bank[:],
                        lhsT=codes[:, i * P : (i + 1) * P].bitcast(FP8X4),
                        lhsT_scale=scales[:, i * P : (i + 1) * P],
                        rhs=h_codes[:].bitcast(FP8X4),
                        rhs_scale=h_scales[:],
                        start=(blk == 0),
                        stop=(blk == 1),
                    )
                width = HALF // 2 if (nh, jh, i) == (1, 1, 3) else HALF
                for j0 in range(0, HALF, width):
                    result = outs.tile([P, width], F32, name="result")
                    nc.scalar.activation(
                        result[:], bank[:, j0 : j0 + width], ACT.Gelu_apprx_tanh, bias=bias[:, nt : nt + 1]
                    )
                    col = jh * HALF + j0
                    nc.sync.dma_start(out=out[nt * P : (nt + 1) * P, col : col + width], in_=result[:])

        grouped = round_wa("wa00", True)
        wa_q[0, 0] = quantise("wa00", grouped)
        for u in range(4):
            part_tab(u, gather_tab(u))
            for c in (2 * u, 2 * u + 1):
                open_bank(0, c)
                pass_wa(0, 0, c, True, False)
        g2s[0] = gather(placed("g2s0", [P, HALF], U8, 98 * KB), tab2_s[:], list2[:, 0:32])
        grouped = round_wa("wa10", True)
        raw["wa11"] = load_rows("wa11", wa, KP, HALF)
        wa_q[1, 0] = quantise("wa10", grouped)
        raw["en00"] = load_en("en00", 0, 0)
        raw["en10"] = load_en("en10", 1, 0)
        for c in range(8):
            pass_wa(1, 0, c, False, False)
        g2w[0] = gather(placed("g2w0", [P, HALF], U32, 30 * KB + 256), tab2_w[:], list2[:, 0:32])
        deal_wb()
        grouped = round_wa("wa01", True)
        for c in range(4):
            pass_wb(0, c, False, True)
            relu_out(0, c)
        g2s[1] = gather(placed("g2s1", [P, HALF], U8, 68 * KB), tab2_s[:], list2[:, 32:64])
        g2w[1] = gather(placed("g2w1", [P, HALF], U32, 66 * KB), tab2_w[:], list2[:, 32:64])
        for c in range(4, 8):
            pass_wb(0, c, False, True)
            relu_out(0, c)
        wa_q[0, 1] = quantise("wa01", grouped)
        raw["en01"] = load_en("en01", 0, 1)
        grouped = round_wa("wa11", False)
        raw["en11"] = load_en("en11", 1, 1)
        wa_q[1, 1] = quantise("wa11", grouped)

        def project_upper(cs):
            for c in cs:
                open_bank(1, c)
                pass_wb(1, c, True, False)
                pass_wa(0, 1, c, False, False)
                pass_wa(1, 1, c, False, True)
                relu_out(1, c)

        turned = psum.tile([P, P], F32, name="bank7")
        nc.tensor.transpose(turned[:], bias_rows[:], identity[:])
        nc.scalar.copy(bias[:], turned[:, 0 : N // P])
        project_upper(range(0, 4))
        for blk in range(2):
            grouped = round_en("en%d0" % blk, False)
            quantise_h(0, blk)
            en_q[blk, 0] = quantise("en%d0" % blk, grouped)
        quantise_h(1, 0)
        project_upper(range(4, 8))
        en_q[0, 1] = quantise("en01", round_en("en01", False))
        grouped = round_en("en11", False)
        quantise_h(1, 1)
        score(0, 0, (0, 1, 2, 3))
        en_q[1, 1] = quantise("en11", grouped)
        score(0, 1, (4, 5, 6, 7))
        score(1, 0, (0, 1, 2, 3))
        score(1, 1, (4, 5, 6, 7))
